import numpy as np
import ml_dtypes


def mxq(x, axis, fmt="e4m3"):
    dtype, down = {"e4m3": (ml_dtypes.float8_e4m3fn, 7), "e5m2": (ml_dtypes.float8_e5m2, 14)}[fmt]
    v = np.moveaxis(np.asarray(x, np.float32).astype(ml_dtypes.bfloat16).astype(np.float64), axis, -1)
    blocks = v.reshape(v.shape[:-1] + (-1, 32))
    amax = np.abs(blocks).max(-1, keepdims=True)
    byte = np.maximum(np.where(amax > 0, np.frexp(amax)[1] - 1 + 127, 0) - down, 1)
    scale = np.exp2(byte - 127.0)
    codes = (blocks / scale).astype(np.float32).astype(dtype).astype(np.float64)
    return np.moveaxis((codes * scale).reshape(v.shape), -1, axis)


WIDE = False


def mx_kscale(k):
    if not WIDE:
        return np.ones(k)
    levels = np.array([10, -10, 5, -5, 0])
    if k % 512:
        return np.exp2(np.random.permutation(np.resize(levels, k // 32))).repeat(32)
    a = np.empty((k // 512, 16))
    for p in range(k // 512):
        a[p, :8] = np.random.permutation(np.resize(levels, 8))
        for g in range(8):
            far = levels[np.abs(levels - a[p, g]) >= 10]
            a[p, g + 8] = far[np.random.randint(len(far))]
    return np.exp2(a.ravel()).repeat(32)


def f64(x):
    return np.asarray(x).astype(np.float64)


def striped(idx):
    return np.tile(idx.reshape(-1, 16).T, (8, 1)).astype(np.uint16)


def unstriped(offs):
    return offs[:16].T.reshape(-1).astype(np.int64)


E2M1 = np.array([0.0, 0.5, 1.0, 1.5, 2.0, 3.0, 4.0, 6.0, -0.0, -0.5, -1.0, -1.5, -2.0, -3.0, -4.0, -6.0])


def pack_weight(w, fmt):
    k, n = w.shape
    w = f64(np.asarray(w, np.float32).astype(ml_dtypes.bfloat16)).reshape(k // 32, 32, n)
    amax = np.abs(w).max(1)
    if fmt == "e4m3":
        byte = np.frexp(amax)[1] - 1 + 127 - 7
    else:
        mant, ex = np.frexp(amax / 6.0)
        byte = np.where(mant > 0.5, ex, ex - 1) + 127
    byte = np.clip(np.where(amax > 0, byte, 1), 1, 254)
    scaled = (w * np.exp2(127.0 - byte)[:, None, :]).reshape(k, n).astype(np.float32)
    by_word = np.ascontiguousarray(scaled.reshape(k // 512, 128, 4, n).transpose(0, 1, 3, 2))
    if fmt == "e4m3":
        words = by_word.astype(ml_dtypes.float8_e4m3fn).view(np.uint8)
    else:
        c = by_word.astype(ml_dtypes.float4_e2m1fn).view(np.uint8) & 0xF
        words = (c[..., 0::2] | (c[..., 1::2] << 4)).reshape(k // 512, 128, 2 * n)
    return np.ascontiguousarray(words), np.ascontiguousarray(byte.astype(np.uint8).reshape(k // 512, 16, n))


def unpack_weight(words, scales, fmt):
    g, _, n = scales.shape
    words = np.ascontiguousarray(words).reshape(g, 128, n, -1)
    if fmt == "e4m3":
        vals = words.view(ml_dtypes.float8_e4m3fn).astype(np.float64)
    else:
        nib = np.empty((g, 128, n, 4), np.uint8)
        nib[..., 0::2] = words & 0xF
        nib[..., 1::2] = words >> 4
        vals = E2M1[nib]
    vals = vals * np.repeat(np.exp2(scales.astype(np.float64) - 127.0), 8, axis=1)[..., None]
    return vals.transpose(0, 1, 3, 2).reshape(g * 512, n)


def gelu(v):
    return 0.5 * v * (1.0 + np.tanh(np.sqrt(2.0 / np.pi) * (v + 0.044715 * v**3)))


K, T, S, K2, H, N = 1024, 4096, 1024, 512, 1024, 512


def setup_inputs():
    n = np.random.standard_normal
    s = mx_kscale(K)[:, None]
    s2 = mx_kscale(K2)[:, None]
    u = mx_kscale(H)[:, None]
    d = {}
    d["tab_words"], d["tab_scales"] = pack_weight(n((K, T)) * s, "e4m3")
    d["offs"] = striped(np.random.permutation(T)[:S])
    d["xs_words"], d["xs_scales"] = pack_weight(n((K2, S)) * s2, "e4m3")
    d["w1"] = (1.4 * n((K, H)) / K ** 0.5 / s).astype(np.float32)
    d["w2_words"], d["w2_scales"] = pack_weight(1.4 * n((K2, H)) / K2 ** 0.5 / s2, "e2m1")
    d["gain"] = (np.exp(0.4 * n(H)) * u[:, 0]).astype(np.float32)
    d["w3"] = (2.0 * n((H, N)) / H ** 0.5 / u).astype(np.float32)
    d["temp"] = np.exp(0.4 * n((N, S))).astype(np.float32)
    return d


def reference(tab_words, tab_scales, offs, xs_words, xs_scales, w1, w2_words, w2_scales, gain, w3, temp):
    v = unpack_weight(tab_words, tab_scales, "e4m3")[:, unstriped(offs)]
    xs = unpack_weight(xs_words, xs_scales, "e4m3")
    w2 = unpack_weight(w2_words, w2_scales, "e2m1")
    a = mxq(f64(w1), 0, "e4m3").T @ v
    b = w2.T @ xs
    near = 1.0 / (1.0 + np.abs(a - b))
    h = f64(gain)[:, None] * near
    y = mxq(f64(w3), 0, "e4m3").T @ mxq(h, 0, "e4m3")
    return y * f64(temp)

@@ -1,0 +1,304 @@
+from contextlib import ExitStack
+
+import concourse.mybir as mybir
+
+K, T, S, K2, H, N = 1024, 4096, 1024, 512, 1024, 512
+FLOPS = 2 * S * (K * H + K2 * H + H * N)
+
+F32 = mybir.dt.float32
+BF16 = mybir.dt.bfloat16
+I32 = mybir.dt.int32
+U32 = mybir.dt.uint32
+U16 = mybir.dt.uint16
+U8 = mybir.dt.uint8
+FP8X4 = mybir.dt.float8_e4m3fn_x4
+FP4X4 = mybir.dt.float4_e2m1fn_x4
+ALU = mybir.AluOpType
+ACT = mybir.ActivationFunctionType
+
+P = 128
+PASS = 512
+BANK = 512
+TINY = 2.0 ** -100
+
+
+def tile_list_coin_closeness_score_kernel(
+    tc, tab_words, tab_scales, offs, xs_words, xs_scales, w1, w2_words, w2_scales, gain, w3, temp, out
+):
+    nc = tc.nc
+    with ExitStack() as ctx:
+        keep = ctx.enter_context(tc.tile_pool(name="keep", bufs=1))
+        ring = ctx.enter_context(tc.tile_pool(name="ring", bufs=2))
+        psum = ctx.enter_context(tc.psum_pool(name="psum", bufs=8))
+
+        def held(shape, dtype, name):
+            return keep.tile(shape, dtype, name=name, align_bytes=64)
+
+        offsets = keep.tile([P, S // 16], U16, name="offsets")
+        tab = [held([P, T], U32, "tab%d" % a) for a in range(2)]
+        tab_sc = held([P, T], U8, "tab_sc")
+        xs = [held([P, BANK], U32, "xs%d" % jh) for jh in range(2)]
+        xs_sc = held([P, S], U8, "xs_sc")
+        w2_raw = [held([P, PASS // 2], I32, "w2_raw%d" % b) for b in range(2)]
+        w2_sc_raw = held([P, H // 4], I32, "w2_sc_raw")
+        w1_raw = [[held([P, 4, PASS], F32, "w1_raw%d%d" % (a, b)) for b in range(2)] for a in range(2)]
+        w3_raw = [held([P, 4, N], F32, "w3_raw%d" % b) for b in range(2)]
+        temp_sb = [held([P, 4, BANK], F32, "temp%d" % jh) for jh in range(2)]
+        gain_sb = held([P, 2, 16], F32, "gain_sb")
+        warm = held([P, 2], F32, "warm")
+
+        nc.vector.memset(warm[:, 0:1], 1.0)
+        nc.scalar.activation(warm[:, 1:2], warm[:, 0:1], ACT.Abs_reciprocal_sqrt)
+        nc.vector.memset(tab_sc[:].bitcast(I32), 0)
+        nc.vector.memset(xs_sc[:].bitcast(I32), 0)
+        nc.vector.memset(w2_sc_raw[:], 0)
+
+        def load_tab(a):
+            nc.sync.dma_start(tab[a][:].bitcast(I32), tab_words[a].rearrange("p t i -> p (t i)").bitcast(I32))
+
+        def load_w1(a, b):
+            rows = w1[PASS * a : PASS * (a + 1), PASS * b : PASS * (b + 1)]
+            nc.sync.dma_start(w1_raw[a][b][:], rows.rearrange("(p j) c -> p j c", j=4))
+
+        def load_xs(jh):
+            words = xs_words[0].rearrange("p c i -> p (c i)").bitcast(I32)
+            nc.sync.dma_start(xs[jh][:].bitcast(I32), words[:, BANK * jh : BANK * (jh + 1)])
+
+        def load_w2(b):
+            nc.sync.dma_start(w2_raw[b][:], w2_words[0].bitcast(I32)[:, PASS // 2 * b : PASS // 2 * (b + 1)])
+
+        load_tab(0)
+        nc.sync.dma_start(offsets[:], offs)
+        gain_rows = gain.rearrange("(b u e) -> u b e", b=2, e=16)
+        for i in range(4):
+            nc.scalar.dma_start(gain_sb[i:P:4, :, 0:13], gain_rows[:, :, i : i + 13])
+        for q in range(4):
+            nc.gpsimd.dma_start(
+                tab_sc[32 * q + 4 : 32 * q + 12, :].bitcast(I32), tab_scales[:, 4 * q : 4 * q + 4, :].bitcast(I32)
+            )
+        for q in range(4):
+            nc.scalar.dma_start(
+                xs_sc[32 * q : 32 * q + 4, :].bitcast(I32), xs_scales[0, 4 * q : 4 * q + 4, :].bitcast(I32)
+            )
+        for q in range(4):
+            nc.scalar.dma_start(w2_sc_raw[32 * q : 32 * q + 4, :], w2_scales[0, 4 * q : 4 * q + 4, :].bitcast(I32))
+        load_w1(0, 0)
+        load_xs(0)
+        load_w2(0)
+        load_tab(1)
+        load_w1(1, 0)
+        load_xs(1)
+        load_w2(1)
+        load_w1(0, 1)
+        load_w1(1, 1)
+        for b in range(2):
+            rows = w3[PASS * b : PASS * (b + 1), :].rearrange("(u t i) n -> t u i n", t=4, i=4)
+            for t in range(4):
+                nc.sync.dma_start(w3_raw[b][:, t, :], rows[t])
+        temp_rows = temp.rearrange("(a p) j -> p a j", p=P)
+        out_rows = out.rearrange("(a p) j -> p a j", p=P)
+        for jh in range(2):
+            nc.sync.dma_start(temp_sb[jh][:], temp_rows[:, :, BANK * jh : BANK * (jh + 1)])
+
+        g = gain_sb[:, :, 0:13:4]
+        sign = held([P, 2, 4], F32, "sign")
+        half = held([P, 2, 4], F32, "half")
+        size = held([P, 2, 4], F32, "size")
+        floor = held([P, 2, 4], F32, "floor")
+        inv = held([P, 2, 4], F32, "inv")
+        nc.vector.tensor_scalar(half[:], g, 0.0, 2.0, op0=ALU.is_ge, op1=ALU.mult)
+        nc.vector.tensor_scalar(sign[:], half[:], -1.0, None, op0=ALU.add)
+        nc.vector.tensor_tensor(size[:], g, sign[:], ALU.mult)
+        nc.vector.tensor_scalar(floor[:], size[:], TINY, None, op0=ALU.max)
+        nc.vector.reciprocal(inv[:], floor[:])
+
+        w2_q = [held([P, PASS // 2], I32, "w2_q%d" % b) for b in range(2)]
+        w2_sc = held([P, H // 4], I32, "w2_sc")
+
+        def deal_w2(b):
+            nc.vector.tensor_copy(
+                w2_q[b][:].rearrange("p (t u e) -> p t u e", t=4, e=2),
+                w2_raw[b][:].rearrange("p (u t e) -> p t u e", t=4, e=2),
+            )
+
+        deal_w2(0)
+        nc.vector.tensor_copy(
+            w2_sc[:].rearrange("p (b t u) -> p b t u", b=2, t=4),
+            w2_sc_raw[:].rearrange("p (b u t) -> p b t u", b=2, t=4),
+        )
+
+        v = [[held([P, BANK], U32, "v%d%d" % (a, jh)) for jh in range(2)] for a in range(2)]
+        v_sc = [held([P, BANK], U8, "v_sc%d" % jh) for jh in range(2)]
+
+        def list_half(jh):
+            return offsets[:, 32 * jh : 32 * (jh + 1)]
+
+        for jh in range(2):
+            nc.vector.tensor_copy(v_sc[jh][:], tab_sc[:].indirect(list_half(jh)))
+        for jh in range(2):
+            nc.vector.tensor_copy(v[0][jh][:], tab[0][:].indirect(list_half(jh)))
+
+        w1_q = [[held([P, PASS], U32, "w1_q%d%d" % (a, b)) for b in range(2)] for a in range(2)]
+        w1_sc = [[held([P, PASS], U8, "w1_sc%d%d" % (a, b)) for b in range(2)] for a in range(2)]
+
+        def quantise_w1(a, b, scalar_slots, by_slot):
+            rounded = ring.tile([P, 4, PASS], BF16, name="rounded", align_bytes=64, bufs=3)
+            src = w1_raw[a][b][:].rearrange("p j (u t i) -> p t u j i", t=4, i=4)
+            dst = rounded[:].rearrange("p t (u i j) -> p t u j i", i=4, j=4)
+            for t in range(4):
+                if t in scalar_slots:
+                    nc.scalar.activation(dst[:, t], src[:, t], ACT.Copy, scale=-1.0)
+                else:
+                    nc.vector.tensor_scalar(dst[:, t], src[:, t], -1.0, None, op0=ALU.mult)
+            step = 1 if by_slot else 4
+            for t in range(0, 4, step):
+                cols = slice(P * t, P * (t + step))
+                nc.vector.quantize_mx(
+                    out=w1_q[a][b][:, cols].bitcast(FP8X4),
+                    scales=w1_sc[a][b][:, cols],
+                    in_=rounded[:, t : t + step, :].rearrange("p t c -> p (t c)"),
+                )
+
+        w3_q = [held([P, N], U32, "w3_q%d" % b) for b in range(2)]
+        w3_sc = [held([P, N], U8, "w3_sc%d" % b) for b in range(2)]
+
+        def quantise_w3(b):
+            rounded = ring.tile([P, 4, PASS], BF16, name="rounded", align_bytes=64, bufs=3)
+            flat = rounded[:].rearrange("p t c -> p (t c)")
+            nc.vector.tensor_tensor(
+                flat.rearrange("p (c i t) -> p c t i", i=4, t=4),
+                w3_raw[b][:].rearrange("p t (c i) -> p c t i", i=4),
+                sign[:, b, :].unsqueeze(1).unsqueeze(3).to_broadcast([P, N // 4, 4, 4]),
+                ALU.mult,
+            )
+            nc.vector.quantize_mx(out=w3_q[b][:].bitcast(FP8X4), scales=w3_sc[b][:], in_=flat)
+
+        def pass_table(bank, a, b, t, jh, start, stop):
+            cols = slice(P * t, P * (t + 1))
+            nc.tensor.matmul_mx(
+                out=bank[:],
+                lhsT=w1_q[a][b][:, cols].bitcast(FP8X4),
+                lhsT_scale=w1_sc[a][b][:, cols],
+                rhs=v[a][jh][:].bitcast(FP8X4),
+                rhs_scale=v_sc[jh][4 + 4 * a : P, :],
+                start=start,
+                stop=stop,
+            )
+
+        def pass_traces(bank, b, t, jh, stop):
+            m = 4 * b + t
+            cols = slice(BANK * jh, BANK * (jh + 1))
+            nc.tensor.matmul_mx(
+                out=bank[:],
+                lhsT=w2_q[b][:].bitcast(U8)[:, 2 * P * t : 2 * P * (t + 1)].bitcast(FP4X4),
+                lhsT_scale=w2_sc[:].bitcast(U8)[:, P * m : P * (m + 1)],
+                rhs=xs[jh][:].bitcast(FP8X4),
+                rhs_scale=xs_sc[:, cols],
+                start=False,
+                stop=stop,
+            )
+
+        quantise_w1(0, 0, (0, 1, 2, 3), False)
+        banks = {}
+        for jh in range(2):
+            for t in range(4):
+                banks[0, jh, t] = psum.tile([P, BANK], F32, name="bank")
+                pass_table(banks[0, jh, t], 0, 0, t, jh, True, False)
+        for t in range(4):
+            pass_traces(banks[0, 0, t], 0, t, 0, False)
+        for jh in range(2):
+            nc.vector.tensor_copy(v[1][jh][:], tab[1][:].indirect(list_half(jh)))
+        quantise_w1(1, 0, (2, 3), True)
+        for t in range(4):
+            pass_table(banks[0, 0, t], 1, 0, t, 0, False, True)
+        for t in range(4):
+            pass_table(banks[0, 1, t], 1, 0, t, 1, False, False)
+            pass_traces(banks[0, 1, t], 0, t, 1, True)
+        deal_w2(1)
+        quantise_w1(0, 1, (), False)
+        quantise_w1(1, 1, (), False)
+
+        h_q = [[held([P, BANK], U32, "h_q%d%d" % (b, jh)) for jh in range(2)] for b in range(2)]
+        h_sc = [[held([P, BANK], U8, "h_sc%d%d" % (b, jh)) for jh in range(2)] for b in range(2)]
+
+        def roots(b, jh, c0, width):
+            root = ring.tile([P, 4, width], F32, name="root", bufs=3)
+            gaps = []
+            for step in range(5):
+                if step < 4:
+                    gap = ring.tile([P, width], F32, name="gap", bufs=4)
+                    nc.scalar.activation(gap[:], banks[b, jh, step][:, c0 : c0 + width], ACT.Abs)
+                    gaps.append(gap)
+                if step > 0:
+                    t = step - 1
+                    c = inv[:, b, t : t + 1]
+                    nc.scalar.activation(root[:, t, :], gaps[t][:], ACT.Abs_reciprocal_sqrt, bias=c, scale=c)
+            return root
+
+        def quantise_h(root, b, jh, c0, r0, width, on_scalar):
+            rounded = ring.tile([P, 4 * width], BF16, name="h_rounded", align_bytes=64, bufs=3)
+            src = root[:, :, r0 : r0 + width].rearrange("p t (c i) -> p c t i", i=4)
+            dst = rounded[:].rearrange("p (c i t) -> p c t i", i=4, t=4)
+            if on_scalar:
+                nc.scalar.activation(dst, src, ACT.Square)
+            else:
+                nc.vector.tensor_tensor(dst, src, src, ALU.mult)
+            nc.vector.quantize_mx(
+                out=h_q[b][jh][:, c0 : c0 + width].bitcast(FP8X4), scales=h_sc[b][jh][:, c0 : c0 + width], in_=rounded[:]
+            )
+
+        def scores(jh, c0, width):
+            per_bank = BANK // width
+            for first in range(0, 4, per_bank):
+                bank = psum.tile([P, BANK], F32, name="bank")
+                for b in range(2):
+                    for s in range(per_bank):
+                        rows = slice(P * (first + s), P * (first + s + 1))
+                        nc.tensor.matmul_mx(
+                            out=bank[:, width * s : width * (s + 1)],
+                            lhsT=w3_q[b][:, rows].bitcast(FP8X4),
+                            lhsT_scale=w3_sc[b][:, rows],
+                            rhs=h_q[b][jh][:, c0 : c0 + width].bitcast(FP8X4),
+                            rhs_scale=h_sc[b][jh][:, c0 : c0 + width],
+                            start=(b == 0 and s == 0),
+                            stop=(b == 1 and s == per_bank - 1),
+                        )
+                result = ring.tile([P, per_bank, width], F32, name="result", bufs=8)
+                nc.vector.tensor_tensor(
+                    result[:],
+                    bank[:].rearrange("p (s c) -> p s c", s=per_bank),
+                    temp_sb[jh][:, first : first + per_bank, c0 : c0 + width],
+                    ALU.mult,
+                )
+                j0 = BANK * jh + c0
+                nc.sync.dma_start(out_rows[:, first : first + per_bank, j0 : j0 + width], result[:])
+
+        def second_block(jh):
+            for t in range(4):
+                banks[1, jh, t] = psum.tile([P, BANK], F32, name="bank")
+                pass_table(banks[1, jh, t], 0, 1, t, jh, True, False)
+                pass_traces(banks[1, jh, t], 1, t, jh, False)
+                pass_table(banks[1, jh, t], 1, 1, t, jh, False, True)
+
+        root = roots(0, 0, 0, BANK)
+        second_block(0)
+        quantise_h(root, 0, 0, 0, 0, 256, False)
+        quantise_h(root, 0, 0, 256, 256, 256, False)
+        quantise_w3(0)
+        root = roots(0, 1, 0, BANK)
+        second_block(1)
+        quantise_h(root, 0, 1, 0, 0, 256, False)
+        quantise_h(root, 0, 1, 256, 256, 256, False)
+        quantise_w3(1)
+        root = roots(1, 0, 0, BANK)
+        quantise_h(root, 1, 0, 0, 0, 256, False)
+        quantise_h(root, 1, 0, 256, 256, 256, True)
+        scores(0, 0, BANK)
+        root = roots(1, 1, 0, 256)
+        last = roots(1, 1, 256, 256)
+        quantise_h(root, 1, 1, 0, 0, 256, True)
+        scores(1, 0, 256)
+        quantise_h(last, 1, 1, 256, 0, 128, True)
+        quantise_h(last, 1, 1, 384, 128, 128, True)
+        scores(1, 256, 128)
+        scores(1, 384, 128)

@@ -45,10 +45,7 @@ def tile_list_coin_closeness_score_kernel(
         w3_raw = [held([P, 4, N], F32, "w3_raw%d" % b) for b in range(2)]
         temp_sb = [held([P, 4, BANK], F32, "temp%d" % jh) for jh in range(2)]
         gain_sb = held([P, 2, 16], F32, "gain_sb")
-        warm = held([P, 2], F32, "warm")
 
-        nc.vector.memset(warm[:, 0:1], 1.0)
-        nc.scalar.activation(warm[:, 1:2], warm[:, 0:1], ACT.Abs_reciprocal_sqrt)
         nc.vector.memset(tab_sc[:].bitcast(I32), 0)
         nc.vector.memset(xs_sc[:].bitcast(I32), 0)
         nc.vector.memset(w2_sc_raw[:], 0)
@@ -67,29 +64,32 @@ def tile_list_coin_closeness_score_kernel(
         def load_w2(b):
             nc.sync.dma_start(w2_raw[b][:], w2_words[0].bitcast(I32)[:, PASS // 2 * b : PASS // 2 * (b + 1)])
 
-        load_tab(0)
-        nc.sync.dma_start(offsets[:], offs)
-        gain_rows = gain.rearrange("(b u e) -> u b e", b=2, e=16)
-        for i in range(4):
-            nc.scalar.dma_start(gain_sb[i:P:4, :, 0:13], gain_rows[:, :, i : i + 13])
+        def load_scales(plane, scales, q):
+            nc.sync.dma_start(plane[32 * q : 32 * q + 4, :], scales[0, 4 * q : 4 * q + 4, :].bitcast(I32))
+
         for q in range(4):
             nc.gpsimd.dma_start(
                 tab_sc[32 * q + 4 : 32 * q + 12, :].bitcast(I32), tab_scales[:, 4 * q : 4 * q + 4, :].bitcast(I32)
             )
-        for q in range(4):
-            nc.scalar.dma_start(
-                xs_sc[32 * q : 32 * q + 4, :].bitcast(I32), xs_scales[0, 4 * q : 4 * q + 4, :].bitcast(I32)
-            )
-        for q in range(4):
-            nc.scalar.dma_start(w2_sc_raw[32 * q : 32 * q + 4, :], w2_scales[0, 4 * q : 4 * q + 4, :].bitcast(I32))
+        nc.sync.dma_start(offsets[:], offs)
+        load_tab(0)
+        gain_rows = gain.rearrange("(b u e) -> u b e", b=2, e=16)
+        for i in range(4):
+            nc.sync.dma_start(gain_sb[i:P:4, :, 0:13], gain_rows[:, :, i : i + 13])
+        for q in range(2):
+            load_scales(w2_sc_raw[:], w2_scales, q)
         load_w1(0, 0)
-        load_xs(0)
-        load_w2(0)
         load_tab(1)
+        for q in range(2, 4):
+            load_scales(w2_sc_raw[:], w2_scales, q)
+        for q in range(4):
+            load_scales(xs_sc[:].bitcast(I32), xs_scales, q)
         load_w1(1, 0)
+        load_w2(0)
+        load_xs(0)
+        load_w1(0, 1)
         load_xs(1)
         load_w2(1)
-        load_w1(0, 1)
         load_w1(1, 1)
         for b in range(2):
             rows = w3[PASS * b : PASS * (b + 1), :].rearrange("(u t i) n -> t u i n", t=4, i=4)
@@ -102,15 +102,19 @@ def tile_list_coin_closeness_score_kernel(
 
         g = gain_sb[:, :, 0:13:4]
         sign = held([P, 2, 4], F32, "sign")
-        half = held([P, 2, 4], F32, "half")
         size = held([P, 2, 4], F32, "size")
         floor = held([P, 2, 4], F32, "floor")
         inv = held([P, 2, 4], F32, "inv")
-        nc.vector.tensor_scalar(half[:], g, 0.0, 2.0, op0=ALU.is_ge, op1=ALU.mult)
-        nc.vector.tensor_scalar(sign[:], half[:], -1.0, None, op0=ALU.add)
-        nc.vector.tensor_tensor(size[:], g, sign[:], ALU.mult)
-        nc.vector.tensor_scalar(floor[:], size[:], TINY, None, op0=ALU.max)
-        nc.vector.reciprocal(inv[:], floor[:])
+        nc.scalar.activation(size[:], g, ACT.Abs)
+        nc.scalar.activation(floor[:], size[:], ACT.Identity, bias=TINY)
+        nc.scalar.activation(sign[:], g, ACT.Sign, bias=TINY)
+        inv_root = held([P, 2, 4], F32, "inv_root")
+        guess = held([P, 2, 4], F32, "guess")
+        product = held([P, 2, 4], F32, "product")
+        nc.scalar.activation(inv_root[:], floor[:], ACT.Abs_reciprocal_sqrt)
+        nc.scalar.activation(guess[:], inv_root[:], ACT.Square)
+        nc.vector.tensor_tensor(product[:], guess[:], floor[:], ALU.mult)
+        nc.vector.scalar_tensor_tensor(inv[:], product[:], 2.0, guess[:], op0=ALU.subtract, op1=ALU.mult)
 
         w2_q = [held([P, PASS // 2], I32, "w2_q%d" % b) for b in range(2)]
         w2_sc = held([P, H // 4], I32, "w2_sc")
@@ -121,43 +125,53 @@ def tile_list_coin_closeness_score_kernel(
                 w2_raw[b][:].rearrange("p (u t e) -> p t u e", t=4, e=2),
             )
 
-        deal_w2(0)
         nc.vector.tensor_copy(
             w2_sc[:].rearrange("p (b t u) -> p b t u", b=2, t=4),
             w2_sc_raw[:].rearrange("p (b u t) -> p b t u", b=2, t=4),
         )
 
-        v = [[held([P, BANK], U32, "v%d%d" % (a, jh)) for jh in range(2)] for a in range(2)]
-        v_sc = [held([P, BANK], U8, "v_sc%d" % jh) for jh in range(2)]
+        v = {}
+        v_sc = {}
 
         def list_half(jh):
             return offsets[:, 32 * jh : 32 * (jh + 1)]
 
-        for jh in range(2):
+        def gather_words(a, jh, tag):
+            v[a, jh] = keep.tile([P, BANK], U32, name="v%d%d" % (a, jh), tag=tag, align_bytes=64)
+            nc.vector.tensor_copy(v[a, jh][:], tab[a][:].indirect(list_half(jh)))
+
+        def gather_scales(jh, tag):
+            v_sc[jh] = keep.tile([P, BANK], U8, name="v_sc%d" % jh, tag=tag, align_bytes=64)
             nc.vector.tensor_copy(v_sc[jh][:], tab_sc[:].indirect(list_half(jh)))
-        for jh in range(2):
-            nc.vector.tensor_copy(v[0][jh][:], tab[0][:].indirect(list_half(jh)))
+
+        gather_words(0, 0, "v00")
+        gather_words(0, 1, "v01")
+        gather_scales(0, "v_sc0")
 
         w1_q = [[held([P, PASS], U32, "w1_q%d%d" % (a, b)) for b in range(2)] for a in range(2)]
         w1_sc = [[held([P, PASS], U8, "w1_sc%d%d" % (a, b)) for b in range(2)] for a in range(2)]
 
         def quantise_w1(a, b, scalar_slots, by_slot):
-            rounded = ring.tile([P, 4, PASS], BF16, name="rounded", align_bytes=64, bufs=3)
+            if by_slot:
+                parts = [keep.tile([P, PASS], BF16, name="slot%d" % t, align_bytes=64)[:] for t in range(4)]
+            else:
+                rounded = ring.tile([P, 4 * PASS], BF16, name="rounded", align_bytes=64, bufs=3)
+                parts = [rounded[:, PASS * t : PASS * (t + 1)] for t in range(4)]
             src = w1_raw[a][b][:].rearrange("p j (u t i) -> p t u j i", t=4, i=4)
-            dst = rounded[:].rearrange("p t (u i j) -> p t u j i", i=4, j=4)
             for t in range(4):
+                dst = parts[t].rearrange("p (u i j) -> p u j i", i=4, j=4)
                 if t in scalar_slots:
-                    nc.scalar.activation(dst[:, t], src[:, t], ACT.Copy, scale=-1.0)
+                    nc.scalar.activation(dst, src[:, t], ACT.Copy, scale=-1.0)
                 else:
-                    nc.vector.tensor_scalar(dst[:, t], src[:, t], -1.0, None, op0=ALU.mult)
-            step = 1 if by_slot else 4
-            for t in range(0, 4, step):
-                cols = slice(P * t, P * (t + step))
-                nc.vector.quantize_mx(
-                    out=w1_q[a][b][:, cols].bitcast(FP8X4),
-                    scales=w1_sc[a][b][:, cols],
-                    in_=rounded[:, t : t + step, :].rearrange("p t c -> p (t c)"),
-                )
+                    nc.vector.tensor_scalar(dst, src[:, t], -1.0, None, op0=ALU.mult)
+            if by_slot:
+                for t in range(4):
+                    cols = slice(P * t, P * (t + 1))
+                    nc.vector.quantize_mx(
+                        out=w1_q[a][b][:, cols].bitcast(FP8X4), scales=w1_sc[a][b][:, cols], in_=parts[t]
+                    )
+            else:
+                nc.vector.quantize_mx(out=w1_q[a][b][:].bitcast(FP8X4), scales=w1_sc[a][b][:], in_=rounded[:])
 
         w3_q = [held([P, N], U32, "w3_q%d" % b) for b in range(2)]
         w3_sc = [held([P, N], U8, "w3_sc%d" % b) for b in range(2)]
@@ -179,13 +193,13 @@ def tile_list_coin_closeness_score_kernel(
                 out=bank[:],
                 lhsT=w1_q[a][b][:, cols].bitcast(FP8X4),
                 lhsT_scale=w1_sc[a][b][:, cols],
-                rhs=v[a][jh][:].bitcast(FP8X4),
+                rhs=v[a, jh][:].bitcast(FP8X4),
                 rhs_scale=v_sc[jh][4 + 4 * a : P, :],
                 start=start,
                 stop=stop,
             )
 
-        def pass_traces(bank, b, t, jh, stop):
+        def pass_traces(bank, b, t, jh, start, stop):
             m = 4 * b + t
             cols = slice(BANK * jh, BANK * (jh + 1))
             nc.tensor.matmul_mx(
@@ -194,35 +208,26 @@ def tile_list_coin_closeness_score_kernel(
                 lhsT_scale=w2_sc[:].bitcast(U8)[:, P * m : P * (m + 1)],
                 rhs=xs[jh][:].bitcast(FP8X4),
                 rhs_scale=xs_sc[:, cols],
-                start=False,
+                start=start,
                 stop=stop,
             )
 
         quantise_w1(0, 0, (0, 1, 2, 3), False)
-        banks = {}
-        for jh in range(2):
-            for t in range(4):
-                banks[0, jh, t] = psum.tile([P, BANK], F32, name="bank")
-                pass_table(banks[0, jh, t], 0, 0, t, jh, True, False)
-        for t in range(4):
-            pass_traces(banks[0, 0, t], 0, t, 0, False)
-        for jh in range(2):
-            nc.vector.tensor_copy(v[1][jh][:], tab[1][:].indirect(list_half(jh)))
-        quantise_w1(1, 0, (2, 3), True)
-        for t in range(4):
-            pass_table(banks[0, 0, t], 1, 0, t, 0, False, True)
-        for t in range(4):
-            pass_table(banks[0, 1, t], 1, 0, t, 1, False, False)
-            pass_traces(banks[0, 1, t], 0, t, 1, True)
-        deal_w2(1)
+        gather_words(1, 0, "v10")
+        quantise_w1(1, 0, (1, 3), True)
+        deal_w2(0)
+        gather_scales(1, "slot2")
+        gather_words(1, 1, "slot3")
         quantise_w1(0, 1, (), False)
+        deal_w2(1)
         quantise_w1(1, 1, (), False)
+        banks = {}
 
         h_q = [[held([P, BANK], U32, "h_q%d%d" % (b, jh)) for jh in range(2)] for b in range(2)]
         h_sc = [[held([P, BANK], U8, "h_sc%d%d" % (b, jh)) for jh in range(2)] for b in range(2)]
 
         def roots(b, jh, c0, width):
-            root = ring.tile([P, 4, width], F32, name="root", bufs=3)
+            root = held([P, 4, width], F32, "root%d%d_%d" % (b, jh, c0))
             gaps = []
             for step in range(5):
                 if step < 4:
@@ -273,31 +278,39 @@ def tile_list_coin_closeness_score_kernel(
                 j0 = BANK * jh + c0
                 nc.sync.dma_start(out_rows[:, first : first + per_bank, j0 : j0 + width], result[:])
 
-        def second_block(jh):
+        def differences(b, jh):
             for t in range(4):
-                banks[1, jh, t] = psum.tile([P, BANK], F32, name="bank")
-                pass_table(banks[1, jh, t], 0, 1, t, jh, True, False)
-                pass_traces(banks[1, jh, t], 1, t, jh, False)
-                pass_table(banks[1, jh, t], 1, 1, t, jh, False, True)
+                bank = psum.tile([P, BANK], F32, name="bank")
+                banks[b, jh, t] = bank
+                if jh == 0:
+                    pass_table(bank, 0, b, t, jh, True, False)
+                    pass_table(bank, 1, b, t, jh, False, False)
+                    pass_traces(bank, b, t, jh, False, True)
+                else:
+                    pass_traces(bank, b, t, jh, True, False)
+                    pass_table(bank, 0, b, t, jh, False, False)
+                    pass_table(bank, 1, b, t, jh, False, True)
 
+        differences(0, 0)
+        differences(0, 1)
         root = roots(0, 0, 0, BANK)
-        second_block(0)
+        differences(1, 0)
         quantise_h(root, 0, 0, 0, 0, 256, False)
         quantise_h(root, 0, 0, 256, 256, 256, False)
         quantise_w3(0)
-        root = roots(0, 1, 0, BANK)
-        second_block(1)
-        quantise_h(root, 0, 1, 0, 0, 256, False)
-        quantise_h(root, 0, 1, 256, 256, 256, False)
         quantise_w3(1)
+        later = roots(0, 1, 0, BANK)
+        differences(1, 1)
         root = roots(1, 0, 0, BANK)
-        quantise_h(root, 1, 0, 0, 0, 256, False)
-        quantise_h(root, 1, 0, 256, 256, 256, True)
+        quantise_h(root, 1, 0, 0, 0, 256, True)
+        quantise_h(root, 1, 0, 256, 256, 256, False)
         scores(0, 0, BANK)
+        quantise_h(later, 0, 1, 0, 0, 256, False)
+        quantise_h(later, 0, 1, 256, 256, 256, False)
         root = roots(1, 1, 0, 256)
-        last = roots(1, 1, 256, 256)
         quantise_h(root, 1, 1, 0, 0, 256, True)
         scores(1, 0, 256)
+        last = roots(1, 1, 256, 256)
         quantise_h(last, 1, 1, 256, 0, 128, True)
         quantise_h(last, 1, 1, 384, 128, 128, True)
         scores(1, 256, 128)

from contextlib import ExitStack

import concourse.mybir as mybir

K, T, S, K2, H, N = 1024, 4096, 1024, 512, 1024, 512
FLOPS = 2 * S * (K * H + K2 * H + H * N)

F32 = mybir.dt.float32
BF16 = mybir.dt.bfloat16
I32 = mybir.dt.int32
U32 = mybir.dt.uint32
U16 = mybir.dt.uint16
U8 = mybir.dt.uint8
FP8X4 = mybir.dt.float8_e4m3fn_x4
FP4X4 = mybir.dt.float4_e2m1fn_x4
ALU = mybir.AluOpType
ACT = mybir.ActivationFunctionType

P = 128
PASS = 512
BANK = 512
TINY = 2.0 ** -100


def tile_list_coin_closeness_score_kernel(
    tc, tab_words, tab_scales, offs, xs_words, xs_scales, w1, w2_words, w2_scales, gain, w3, temp, out
):
    nc = tc.nc
    with ExitStack() as ctx:
        keep = ctx.enter_context(tc.tile_pool(name="keep", bufs=1))
        ring = ctx.enter_context(tc.tile_pool(name="ring", bufs=2))
        psum = ctx.enter_context(tc.psum_pool(name="psum", bufs=8))

        def held(shape, dtype, name):
            return keep.tile(shape, dtype, name=name, align_bytes=64)

        offsets = keep.tile([P, S // 16], U16, name="offsets")
        tab = [held([P, T], U32, "tab%d" % a) for a in range(2)]
        tab_sc = held([P, T], U8, "tab_sc")
        xs = [held([P, BANK], U32, "xs%d" % jh) for jh in range(2)]
        xs_sc = held([P, S], U8, "xs_sc")
        w2_raw = [held([P, PASS // 2], I32, "w2_raw%d" % b) for b in range(2)]
        w2_sc_raw = held([P, H // 4], I32, "w2_sc_raw")
        w1_raw = [[held([P, 4, PASS], F32, "w1_raw%d%d" % (a, b)) for b in range(2)] for a in range(2)]
        w3_raw = [held([P, 4, N], F32, "w3_raw%d" % b) for b in range(2)]
        temp_sb = [held([P, 4, BANK], F32, "temp%d" % jh) for jh in range(2)]
        gain_sb = held([P, 2, 16], F32, "gain_sb")

        nc.vector.memset(tab_sc[:].bitcast(I32), 0)
        nc.vector.memset(xs_sc[:].bitcast(I32), 0)
        nc.vector.memset(w2_sc_raw[:], 0)

        def load_tab(a):
            nc.sync.dma_start(tab[a][:].bitcast(I32), tab_words[a].rearrange("p t i -> p (t i)").bitcast(I32))

        def load_w1(a, b):
            rows = w1[PASS * a : PASS * (a + 1), PASS * b : PASS * (b + 1)]
            nc.sync.dma_start(w1_raw[a][b][:], rows.rearrange("(p j) c -> p j c", j=4))

        def load_xs(jh):
            words = xs_words[0].rearrange("p c i -> p (c i)").bitcast(I32)
            nc.sync.dma_start(xs[jh][:].bitcast(I32), words[:, BANK * jh : BANK * (jh + 1)])

        def load_w2(b):
            nc.sync.dma_start(w2_raw[b][:], w2_words[0].bitcast(I32)[:, PASS // 2 * b : PASS // 2 * (b + 1)])

        def load_scales(plane, scales, q):
            nc.sync.dma_start(plane[32 * q : 32 * q + 4, :], scales[0, 4 * q : 4 * q + 4, :].bitcast(I32))

        for q in range(4):
            nc.gpsimd.dma_start(
                tab_sc[32 * q + 4 : 32 * q + 12, :].bitcast(I32), tab_scales[:, 4 * q : 4 * q + 4, :].bitcast(I32)
            )
        nc.sync.dma_start(offsets[:], offs)
        load_tab(0)
        gain_rows = gain.rearrange("(b u e) -> u b e", b=2, e=16)
        for i in range(4):
            nc.sync.dma_start(gain_sb[i:P:4, :, 0:13], gain_rows[:, :, i : i + 13])
        for q in range(2):
            load_scales(w2_sc_raw[:], w2_scales, q)
        load_w1(0, 0)
        load_tab(1)
        for q in range(2, 4):
            load_scales(w2_sc_raw[:], w2_scales, q)
        for q in range(4):
            load_scales(xs_sc[:].bitcast(I32), xs_scales, q)
        load_w1(1, 0)
        load_w2(0)
        load_xs(0)
        load_w1(0, 1)
        load_xs(1)
        load_w2(1)
        load_w1(1, 1)
        for b in range(2):
            rows = w3[PASS * b : PASS * (b + 1), :].rearrange("(u t i) n -> t u i n", t=4, i=4)
            for t in range(4):
                nc.sync.dma_start(w3_raw[b][:, t, :], rows[t])
        temp_rows = temp.rearrange("(a p) j -> p a j", p=P)
        out_rows = out.rearrange("(a p) j -> p a j", p=P)
        for jh in range(2):
            nc.sync.dma_start(temp_sb[jh][:], temp_rows[:, :, BANK * jh : BANK * (jh + 1)])

        g = gain_sb[:, :, 0:13:4]
        sign = held([P, 2, 4], F32, "sign")
        size = held([P, 2, 4], F32, "size")
        floor = held([P, 2, 4], F32, "floor")
        inv = held([P, 2, 4], F32, "inv")
        nc.scalar.activation(size[:], g, ACT.Abs)
        nc.scalar.activation(floor[:], size[:], ACT.Identity, bias=TINY)
        nc.scalar.activation(sign[:], g, ACT.Sign, bias=TINY)
        inv_root = held([P, 2, 4], F32, "inv_root")
        guess = held([P, 2, 4], F32, "guess")
        product = held([P, 2, 4], F32, "product")
        nc.scalar.activation(inv_root[:], floor[:], ACT.Abs_reciprocal_sqrt)
        nc.scalar.activation(guess[:], inv_root[:], ACT.Square)
        nc.vector.tensor_tensor(product[:], guess[:], floor[:], ALU.mult)
        nc.vector.scalar_tensor_tensor(inv[:], product[:], 2.0, guess[:], op0=ALU.subtract, op1=ALU.mult)

        w2_q = [held([P, PASS // 2], I32, "w2_q%d" % b) for b in range(2)]
        w2_sc = held([P, H // 4], I32, "w2_sc")

        def deal_w2(b):
            nc.vector.tensor_copy(
                w2_q[b][:].rearrange("p (t u e) -> p t u e", t=4, e=2),
                w2_raw[b][:].rearrange("p (u t e) -> p t u e", t=4, e=2),
            )

        nc.vector.tensor_copy(
            w2_sc[:].rearrange("p (b t u) -> p b t u", b=2, t=4),
            w2_sc_raw[:].rearrange("p (b u t) -> p b t u", b=2, t=4),
        )

        v = {}
        v_sc = {}

        def list_half(jh):
            return offsets[:, 32 * jh : 32 * (jh + 1)]

        def gather_words(a, jh, tag):
            v[a, jh] = keep.tile([P, BANK], U32, name="v%d%d" % (a, jh), tag=tag, align_bytes=64)
            nc.vector.tensor_copy(v[a, jh][:], tab[a][:].indirect(list_half(jh)))

        def gather_scales(jh, tag):
            v_sc[jh] = keep.tile([P, BANK], U8, name="v_sc%d" % jh, tag=tag, align_bytes=64)
            nc.vector.tensor_copy(v_sc[jh][:], tab_sc[:].indirect(list_half(jh)))

        gather_words(0, 0, "v00")
        gather_words(0, 1, "v01")
        gather_scales(0, "v_sc0")

        w1_q = [[held([P, PASS], U32, "w1_q%d%d" % (a, b)) for b in range(2)] for a in range(2)]
        w1_sc = [[held([P, PASS], U8, "w1_sc%d%d" % (a, b)) for b in range(2)] for a in range(2)]

        def quantise_w1(a, b, scalar_slots, by_slot):
            if by_slot:
                parts = [keep.tile([P, PASS], BF16, name="slot%d" % t, align_bytes=64)[:] for t in range(4)]
            else:
                rounded = ring.tile([P, 4 * PASS], BF16, name="rounded", align_bytes=64, bufs=3)
                parts = [rounded[:, PASS * t : PASS * (t + 1)] for t in range(4)]
            src = w1_raw[a][b][:].rearrange("p j (u t i) -> p t u j i", t=4, i=4)
            for t in range(4):
                dst = parts[t].rearrange("p (u i j) -> p u j i", i=4, j=4)
                if t in scalar_slots:
                    nc.scalar.activation(dst, src[:, t], ACT.Copy, scale=-1.0)
                else:
                    nc.vector.tensor_scalar(dst, src[:, t], -1.0, None, op0=ALU.mult)
            if by_slot:
                for t in range(4):
                    cols = slice(P * t, P * (t + 1))
                    nc.vector.quantize_mx(
                        out=w1_q[a][b][:, cols].bitcast(FP8X4), scales=w1_sc[a][b][:, cols], in_=parts[t]
                    )
            else:
                nc.vector.quantize_mx(out=w1_q[a][b][:].bitcast(FP8X4), scales=w1_sc[a][b][:], in_=rounded[:])

        w3_q = [held([P, N], U32, "w3_q%d" % b) for b in range(2)]
        w3_sc = [held([P, N], U8, "w3_sc%d" % b) for b in range(2)]

        def quantise_w3(b):
            rounded = ring.tile([P, 4, PASS], BF16, name="rounded", align_bytes=64, bufs=3)
            flat = rounded[:].rearrange("p t c -> p (t c)")
            nc.vector.tensor_tensor(
                flat.rearrange("p (c i t) -> p c t i", i=4, t=4),
                w3_raw[b][:].rearrange("p t (c i) -> p c t i", i=4),
                sign[:, b, :].unsqueeze(1).unsqueeze(3).to_broadcast([P, N // 4, 4, 4]),
                ALU.mult,
            )
            nc.vector.quantize_mx(out=w3_q[b][:].bitcast(FP8X4), scales=w3_sc[b][:], in_=flat)

        def pass_table(bank, a, b, t, jh, start, stop):
            cols = slice(P * t, P * (t + 1))
            nc.tensor.matmul_mx(
                out=bank[:],
                lhsT=w1_q[a][b][:, cols].bitcast(FP8X4),
                lhsT_scale=w1_sc[a][b][:, cols],
                rhs=v[a, jh][:].bitcast(FP8X4),
                rhs_scale=v_sc[jh][4 + 4 * a : P, :],
                start=start,
                stop=stop,
            )

        def pass_traces(bank, b, t, jh, start, stop):
            m = 4 * b + t
            cols = slice(BANK * jh, BANK * (jh + 1))
            nc.tensor.matmul_mx(
                out=bank[:],
                lhsT=w2_q[b][:].bitcast(U8)[:, 2 * P * t : 2 * P * (t + 1)].bitcast(FP4X4),
                lhsT_scale=w2_sc[:].bitcast(U8)[:, P * m : P * (m + 1)],
                rhs=xs[jh][:].bitcast(FP8X4),
                rhs_scale=xs_sc[:, cols],
                start=start,
                stop=stop,
            )

        quantise_w1(0, 0, (0, 1, 2, 3), False)
        gather_words(1, 0, "v10")
        quantise_w1(1, 0, (1, 3), True)
        deal_w2(0)
        gather_scales(1, "slot2")
        gather_words(1, 1, "slot3")
        quantise_w1(0, 1, (), False)
        deal_w2(1)
        quantise_w1(1, 1, (), False)
        banks = {}

        h_q = [[held([P, BANK], U32, "h_q%d%d" % (b, jh)) for jh in range(2)] for b in range(2)]
        h_sc = [[held([P, BANK], U8, "h_sc%d%d" % (b, jh)) for jh in range(2)] for b in range(2)]

        def roots(b, jh, c0, width):
            root = held([P, 4, width], F32, "root%d%d_%d" % (b, jh, c0))
            gaps = []
            for step in range(5):
                if step < 4:
                    gap = ring.tile([P, width], F32, name="gap", bufs=4)
                    nc.scalar.activation(gap[:], banks[b, jh, step][:, c0 : c0 + width], ACT.Abs)
                    gaps.append(gap)
                if step > 0:
                    t = step - 1
                    c = inv[:, b, t : t + 1]
                    nc.scalar.activation(root[:, t, :], gaps[t][:], ACT.Abs_reciprocal_sqrt, bias=c, scale=c)
            return root

        def quantise_h(root, b, jh, c0, r0, width, on_scalar):
            rounded = ring.tile([P, 4 * width], BF16, name="h_rounded", align_bytes=64, bufs=3)
            src = root[:, :, r0 : r0 + width].rearrange("p t (c i) -> p c t i", i=4)
            dst = rounded[:].rearrange("p (c i t) -> p c t i", i=4, t=4)
            if on_scalar:
                nc.scalar.activation(dst, src, ACT.Square)
            else:
                nc.vector.tensor_tensor(dst, src, src, ALU.mult)
            nc.vector.quantize_mx(
                out=h_q[b][jh][:, c0 : c0 + width].bitcast(FP8X4), scales=h_sc[b][jh][:, c0 : c0 + width], in_=rounded[:]
            )

        def scores(jh, c0, width):
            per_bank = BANK // width
            for first in range(0, 4, per_bank):
                bank = psum.tile([P, BANK], F32, name="bank")
                for b in range(2):
                    for s in range(per_bank):
                        rows = slice(P * (first + s), P * (first + s + 1))
                        nc.tensor.matmul_mx(
                            out=bank[:, width * s : width * (s + 1)],
                            lhsT=w3_q[b][:, rows].bitcast(FP8X4),
                            lhsT_scale=w3_sc[b][:, rows],
                            rhs=h_q[b][jh][:, c0 : c0 + width].bitcast(FP8X4),
                            rhs_scale=h_sc[b][jh][:, c0 : c0 + width],
                            start=(b == 0 and s == 0),
                            stop=(b == 1 and s == per_bank - 1),
                        )
                result = ring.tile([P, per_bank, width], F32, name="result", bufs=8)
                nc.vector.tensor_tensor(
                    result[:],
                    bank[:].rearrange("p (s c) -> p s c", s=per_bank),
                    temp_sb[jh][:, first : first + per_bank, c0 : c0 + width],
                    ALU.mult,
                )
                j0 = BANK * jh + c0
                nc.sync.dma_start(out_rows[:, first : first + per_bank, j0 : j0 + width], result[:])

        def differences(b, jh):
            for t in range(4):
                bank = psum.tile([P, BANK], F32, name="bank")
                banks[b, jh, t] = bank
                if jh == 0:
                    pass_table(bank, 0, b, t, jh, True, False)
                    pass_table(bank, 1, b, t, jh, False, False)
                    pass_traces(bank, b, t, jh, False, True)
                else:
                    pass_traces(bank, b, t, jh, True, False)
                    pass_table(bank, 0, b, t, jh, False, False)
                    pass_table(bank, 1, b, t, jh, False, True)

        differences(0, 0)
        differences(0, 1)
        root = roots(0, 0, 0, BANK)
        differences(1, 0)
        quantise_h(root, 0, 0, 0, 0, 256, False)
        quantise_h(root, 0, 0, 256, 256, 256, False)
        quantise_w3(0)
        quantise_w3(1)
        later = roots(0, 1, 0, BANK)
        differences(1, 1)
        root = roots(1, 0, 0, BANK)
        quantise_h(root, 1, 0, 0, 0, 256, True)
        quantise_h(root, 1, 0, 256, 256, 256, False)
        scores(0, 0, BANK)
        quantise_h(later, 0, 1, 0, 0, 256, False)
        quantise_h(later, 0, 1, 256, 256, 256, False)
        root = roots(1, 1, 0, 256)
        quantise_h(root, 1, 1, 0, 0, 256, True)
        scores(1, 0, 256)
        last = roots(1, 1, 256, 256)
        quantise_h(last, 1, 1, 256, 0, 128, True)
        quantise_h(last, 1, 1, 384, 128, 128, True)
        scores(1, 256, 128)
        scores(1, 384, 128)
